import numpy as np, ml_dtypes
CORES = [32,33,34,35,36,37,38,39,40,41,42,43,44,45,46,47]
N = 16
def setup_inputs(rng):
    return {"x": rng.standard_normal((N, 128, 64), dtype=np.float32).astype(ml_dtypes.bfloat16)}
def reference(x):
    s = x.max(axis=0)
    b = 64 // N
    return {"y": np.stack([s[:, r * b:(r + 1) * b] for r in range(N)])}

@@ -1,0 +1,63 @@
+from concourse.bass import DstId, RemoteDMATransfer
+
+GATE = (2, 3, 6, 7)
+
+SCRATCH = {
+    "xd": ("dram", [512, 16], "bfloat16"),
+    "gath": ("dram", [1024, 16], "bfloat16"),
+    "part": ("dram", [128, 16], "bfloat16"),
+    "sfull": ("dram", [512, 16], "bfloat16"),
+}
+SEMAPHORES = ["local", "sent", "a1", "a2", "a3"]
+
+
+def blk(t, i):
+    return t[128 * i:128 * (i + 1), :]
+
+
+def rank_program(g, core, T, topo):
+    rank = T.rank_of(core)
+    if rank is None:
+        return
+    base = topo.chip(core) * 8
+    k = core % 8
+    sem = T.sem
+
+    def did(c):
+        rid, pid, se = topo.addr(c)
+        return DstId(rid=rid, pnc=pid)
+
+    g.dma_start(out=T.xd[:], in_=T.x[:]).then_inc(sem.local, 16)
+    g.wait_ge(sem.local, 16)
+
+    tr = []
+    for q, gk in enumerate(GATE):
+        if gk != k:
+            tr.append(RemoteDMATransfer(dst_ids=[did(base + gk)], dma_engine_mask=0xF << (4 * q), remote_sem=sem.a1,
+                                        src=blk(T.xd, q), dst=blk(T.gath, k), alu_op=0))
+    g.remote_dma_fused(tr, local_sem=sem.sent)
+    sent = 4 * len(tr)
+
+    if k in GATE:
+        q = GATE.index(k)
+        mate = core ^ 8
+        srcs = [blk(T.xd, q)] + [blk(T.gath, j) for j in range(8) if j != k]
+        g.wait_ge(sem.a1, 28)
+        g.remote_dma_fused([RemoteDMATransfer(dst_ids=[did(mate)], dma_engine_mask=0x00FF, remote_sem=sem.a2,
+                                              srcs=srcs, dsts=[T.part[:]], alu_op=2)], local_sem=sem.sent)
+        sent += 8
+        g.wait_ge(sem.a2, 8)
+        others = [base + j for j in range(8) if j != k]
+        g.remote_dma_fused([
+            RemoteDMATransfer(dst_ids=[did(mate)], dma_engine_mask=0x00FF, remote_sem=sem.a3,
+                              srcs=srcs + [T.part[:]], dsts=[blk(T.sfull, q)], alu_op=2),
+            RemoteDMATransfer(dst_ids=[did(c) for c in others], dma_engine_mask=0xFF00, remote_sem=sem.a3,
+                              srcs=srcs + [T.part[:]], dsts=[blk(T.sfull, q) for c in others], alu_op=2),
+        ], local_sem=sem.sent)
+        sent += 16
+
+    g.wait_ge(sem.a3, 32)
+    c0 = 4 * (rank % 4)
+    g.dma_start(out=T.y[:], in_=T.sfull[rank // 4::4, c0:c0 + 4]).then_inc(sem.local, 16)
+    g.wait_ge(sem.local, 32)
+    g.wait_ge(sem.sent, sent)

@@ -1,11 +1,13 @@
 from concourse.bass import DstId, RemoteDMATransfer
 
 GATE = (2, 3, 6, 7)
+PLAIN = (0, 1, 4, 5)
 
 SCRATCH = {
     "xd": ("dram", [512, 16], "bfloat16"),
     "gath": ("dram", [1024, 16], "bfloat16"),
-    "part": ("dram", [128, 16], "bfloat16"),
+    "pown": ("dram", [128, 16], "bfloat16"),
+    "pmate": ("dram", [128, 16], "bfloat16"),
     "sfull": ("dram", [512, 16], "bfloat16"),
 }
 SEMAPHORES = ["local", "sent", "a1", "a2", "a3"]
@@ -15,11 +17,16 @@ def blk(t, i):
     return t[128 * i:128 * (i + 1), :]
 
 
+def finishers(q):
+    return PLAIN[q], GATE[q ^ 1]
+
+
 def rank_program(g, core, T, topo):
     rank = T.rank_of(core)
     if rank is None:
         return
     base = topo.chip(core) * 8
+    mbase = base ^ 8
     k = core % 8
     sem = T.sem
 
@@ -40,23 +47,28 @@ def rank_program(g, core, T, topo):
 
     if k in GATE:
         q = GATE.index(k)
-        mate = core ^ 8
+        fin = finishers(q)
         srcs = [blk(T.xd, q)] + [blk(T.gath, j) for j in range(8) if j != k]
         g.wait_ge(sem.a1, 28)
-        g.remote_dma_fused([RemoteDMATransfer(dst_ids=[did(mate)], dma_engine_mask=0x00FF, remote_sem=sem.a2,
-                                              srcs=srcs, dsts=[T.part[:]], alu_op=2)], local_sem=sem.sent)
-        sent += 8
-        g.wait_ge(sem.a2, 8)
-        others = [base + j for j in range(8) if j != k]
         g.remote_dma_fused([
-            RemoteDMATransfer(dst_ids=[did(mate)], dma_engine_mask=0x00FF, remote_sem=sem.a3,
-                              srcs=srcs + [T.part[:]], dsts=[blk(T.sfull, q)], alu_op=2),
-            RemoteDMATransfer(dst_ids=[did(c) for c in others], dma_engine_mask=0xFF00, remote_sem=sem.a3,
-                              srcs=srcs + [T.part[:]], dsts=[blk(T.sfull, q) for c in others], alu_op=2),
+            RemoteDMATransfer(dst_ids=[did(mbase + f) for f in fin], dma_engine_mask=0x00FF, remote_sem=sem.a2,
+                              srcs=srcs, dsts=[T.pmate[:] for f in fin], alu_op=2),
+            RemoteDMATransfer(dst_ids=[did(base + f) for f in fin], dma_engine_mask=0xFF00, remote_sem=sem.a2,
+                              srcs=srcs, dsts=[T.pown[:] for f in fin], alu_op=2),
         ], local_sem=sem.sent)
         sent += 16
 
-    g.wait_ge(sem.a3, 32)
+    q = PLAIN.index(k) if k in PLAIN else GATE.index(k) ^ 1
+    f1, f2 = finishers(q)
+    rest = [j for j in range(8) if j != f1 and j != f2]
+    to = [f2] + rest[0:3] if k == f1 else [f1] + rest[3:6]
+    g.wait_ge(sem.a2, 16)
+    g.remote_dma_fused([RemoteDMATransfer(dst_ids=[did(base + j) for j in to], dma_engine_mask=0xFFFF,
+                                          remote_sem=sem.a3, srcs=[T.pown[:], T.pmate[:]],
+                                          dsts=[blk(T.sfull, q) for j in to], alu_op=2)], local_sem=sem.sent)
+    sent += 16
+
+    g.wait_ge(sem.a3, 64)
     c0 = 4 * (rank % 4)
     g.dma_start(out=T.y[:], in_=T.sfull[rank // 4::4, c0:c0 + 4]).then_inc(sem.local, 16)
     g.wait_ge(sem.local, 32)

@@ -4,11 +4,11 @@ GATE = (2, 3, 6, 7)
 PLAIN = (0, 1, 4, 5)
 
 SCRATCH = {
-    "xd": ("dram", [512, 16], "bfloat16"),
-    "gath": ("dram", [1024, 16], "bfloat16"),
-    "pown": ("dram", [128, 16], "bfloat16"),
-    "pmate": ("dram", [128, 16], "bfloat16"),
-    "sfull": ("dram", [512, 16], "bfloat16"),
+    "xh": ("dram", [1024, 8], "bfloat16"),
+    "gath": ("dram", [1024, 8], "bfloat16"),
+    "pown": ("dram", [128, 8], "bfloat16"),
+    "pmate": ("dram", [128, 8], "bfloat16"),
+    "sh": ("dram", [512, 8], "bfloat16"),
 }
 SEMAPHORES = ["local", "sent", "a1", "a2", "a3"]
 
@@ -18,7 +18,7 @@ def blk(t, i):
 
 
 def finishers(q):
-    return PLAIN[q], GATE[q ^ 1]
+    return GATE[q], PLAIN[q ^ 1]
 
 
 def rank_program(g, core, T, topo):
@@ -28,48 +28,54 @@ def rank_program(g, core, T, topo):
     base = topo.chip(core) * 8
     mbase = base ^ 8
     k = core % 8
+    own = rank // 8
     sem = T.sem
 
     def did(c):
         rid, pid, se = topo.addr(c)
         return DstId(rid=rid, pnc=pid)
 
-    g.dma_start(out=T.xd[:], in_=T.x[:]).then_inc(sem.local, 16)
-    g.wait_ge(sem.local, 16)
+    def piece(j):
+        return blk(T.xh, 4 * (1 - own) + GATE.index(j)) if j in GATE else blk(T.xh, 4 * own + PLAIN.index(j))
 
-    tr = []
-    for q, gk in enumerate(GATE):
-        if gk != k:
-            tr.append(RemoteDMATransfer(dst_ids=[did(base + gk)], dma_engine_mask=0xF << (4 * q), remote_sem=sem.a1,
-                                        src=blk(T.xd, q), dst=blk(T.gath, k), alu_op=0))
-    g.remote_dma_fused(tr, local_sem=sem.sent)
-    sent = 4 * len(tr)
+    g.dma_start(out=T.xh[0:512, :], in_=T.x[:, 0:32]).then_inc(sem.local, 16)
+    g.dma_start(out=T.xh[512:1024, :], in_=T.x[:, 32:64]).then_inc(sem.local, 16)
+    g.wait_ge(sem.local, 32)
 
+    others = [j for j in range(8) if j != k]
+    g.remote_dma_fused([RemoteDMATransfer(dst_ids=[did(base + j)], dma_engine_mask=0x3 << (2 * i), remote_sem=sem.a1,
+                                          src=piece(j), dst=blk(T.gath, k), alu_op=0)
+                        for i, j in enumerate(others)], local_sem=sem.sent)
+    sent = 14
+
+    srcs = [piece(k)] + [blk(T.gath, j) for j in others]
+    g.wait_ge(sem.a1, 14)
     if k in GATE:
-        q = GATE.index(k)
-        fin = finishers(q)
-        srcs = [blk(T.xd, q)] + [blk(T.gath, j) for j in range(8) if j != k]
-        g.wait_ge(sem.a1, 28)
-        g.remote_dma_fused([
-            RemoteDMATransfer(dst_ids=[did(mbase + f) for f in fin], dma_engine_mask=0x00FF, remote_sem=sem.a2,
-                              srcs=srcs, dsts=[T.pmate[:] for f in fin], alu_op=2),
-            RemoteDMATransfer(dst_ids=[did(base + f) for f in fin], dma_engine_mask=0xFF00, remote_sem=sem.a2,
-                              srcs=srcs, dsts=[T.pown[:] for f in fin], alu_op=2),
-        ], local_sem=sem.sent)
+        fin = finishers(GATE.index(k))
+        g.remote_dma_fused([RemoteDMATransfer(dst_ids=[did(mbase + f) for f in fin], dma_engine_mask=0x00FF,
+                                              remote_sem=sem.a2, srcs=srcs, dsts=[T.pmate[:] for f in fin],
+                                              alu_op=2)], local_sem=sem.sent)
+        sent += 8
+    else:
+        fin = finishers(PLAIN.index(k))
+        g.remote_dma_fused([RemoteDMATransfer(dst_ids=[did(base + f) for f in fin], dma_engine_mask=0xFFFF,
+                                              remote_sem=sem.a2, srcs=srcs, dsts=[T.pown[:] for f in fin],
+                                              alu_op=2)], local_sem=sem.sent)
         sent += 16
 
-    q = PLAIN.index(k) if k in PLAIN else GATE.index(k) ^ 1
+    q = GATE.index(k) if k in GATE else PLAIN.index(k) ^ 1
     f1, f2 = finishers(q)
     rest = [j for j in range(8) if j != f1 and j != f2]
     to = [f2] + rest[0:3] if k == f1 else [f1] + rest[3:6]
-    g.wait_ge(sem.a2, 16)
+    g.wait_ge(sem.a2, 24)
     g.remote_dma_fused([RemoteDMATransfer(dst_ids=[did(base + j) for j in to], dma_engine_mask=0xFFFF,
                                           remote_sem=sem.a3, srcs=[T.pown[:], T.pmate[:]],
-                                          dsts=[blk(T.sfull, q) for j in to], alu_op=2)], local_sem=sem.sent)
+                                          dsts=[blk(T.sh, q) for j in to], alu_op=2)], local_sem=sem.sent)
     sent += 16
 
     g.wait_ge(sem.a3, 64)
-    c0 = 4 * (rank % 4)
-    g.dma_start(out=T.y[:], in_=T.sfull[rank // 4::4, c0:c0 + 4]).then_inc(sem.local, 16)
-    g.wait_ge(sem.local, 32)
+    r8 = rank % 8
+    c0 = 4 * (r8 % 2)
+    g.dma_start(out=T.y[:], in_=T.sh[r8 // 2::4, c0:c0 + 4]).then_inc(sem.local, 16)
+    g.wait_ge(sem.local, 48)
     g.wait_ge(sem.sent, sent)

from concourse.bass import DstId, RemoteDMATransfer

GATE = (2, 3, 6, 7)
PLAIN = (0, 1, 4, 5)

SCRATCH = {
    "xh": ("dram", [1024, 8], "bfloat16"),
    "gath": ("dram", [1024, 8], "bfloat16"),
    "pown": ("dram", [128, 8], "bfloat16"),
    "pmate": ("dram", [128, 8], "bfloat16"),
    "sh": ("dram", [512, 8], "bfloat16"),
}
SEMAPHORES = ["local", "sent", "a1", "a2", "a3"]


def blk(t, i):
    return t[128 * i:128 * (i + 1), :]


def finishers(q):
    return GATE[q], PLAIN[q ^ 1]


def rank_program(g, core, T, topo):
    rank = T.rank_of(core)
    if rank is None:
        return
    base = topo.chip(core) * 8
    mbase = base ^ 8
    k = core % 8
    own = rank // 8
    sem = T.sem

    def did(c):
        rid, pid, se = topo.addr(c)
        return DstId(rid=rid, pnc=pid)

    def piece(j):
        return blk(T.xh, 4 * (1 - own) + GATE.index(j)) if j in GATE else blk(T.xh, 4 * own + PLAIN.index(j))

    g.dma_start(out=T.xh[0:512, :], in_=T.x[:, 0:32]).then_inc(sem.local, 16)
    g.dma_start(out=T.xh[512:1024, :], in_=T.x[:, 32:64]).then_inc(sem.local, 16)
    g.wait_ge(sem.local, 32)

    others = [j for j in range(8) if j != k]
    g.remote_dma_fused([RemoteDMATransfer(dst_ids=[did(base + j)], dma_engine_mask=0x3 << (2 * i), remote_sem=sem.a1,
                                          src=piece(j), dst=blk(T.gath, k), alu_op=0)
                        for i, j in enumerate(others)], local_sem=sem.sent)
    sent = 14

    srcs = [piece(k)] + [blk(T.gath, j) for j in others]
    g.wait_ge(sem.a1, 14)
    if k in GATE:
        fin = finishers(GATE.index(k))
        g.remote_dma_fused([RemoteDMATransfer(dst_ids=[did(mbase + f) for f in fin], dma_engine_mask=0x00FF,
                                              remote_sem=sem.a2, srcs=srcs, dsts=[T.pmate[:] for f in fin],
                                              alu_op=2)], local_sem=sem.sent)
        sent += 8
    else:
        fin = finishers(PLAIN.index(k))
        g.remote_dma_fused([RemoteDMATransfer(dst_ids=[did(base + f) for f in fin], dma_engine_mask=0xFFFF,
                                              remote_sem=sem.a2, srcs=srcs, dsts=[T.pown[:] for f in fin],
                                              alu_op=2)], local_sem=sem.sent)
        sent += 16

    q = GATE.index(k) if k in GATE else PLAIN.index(k) ^ 1
    f1, f2 = finishers(q)
    rest = [j for j in range(8) if j != f1 and j != f2]
    to = [f2] + rest[0:3] if k == f1 else [f1] + rest[3:6]
    g.wait_ge(sem.a2, 24)
    g.remote_dma_fused([RemoteDMATransfer(dst_ids=[did(base + j) for j in to], dma_engine_mask=0xFFFF,
                                          remote_sem=sem.a3, srcs=[T.pown[:], T.pmate[:]],
                                          dsts=[blk(T.sh, q) for j in to], alu_op=2)], local_sem=sem.sent)
    sent += 16

    g.wait_ge(sem.a3, 64)
    r8 = rank % 8
    c0 = 4 * (r8 % 2)
    g.dma_start(out=T.y[:], in_=T.sh[r8 // 2::4, c0:c0 + 4]).then_inc(sem.local, 16)
    g.wait_ge(sem.local, 48)
    g.wait_ge(sem.sent, sent)
